import numpy as np
CORES = [5,13,21,29,37,45,53,61,69,77,85,93,101,109,117,125]
N = 16
T = 4
ROUTE = [[[4,1,13],[8,3,14],[14,2,11],[1,2,4]],[[0,7,2],[13,15,2],[0,13,7],[15,2,7]],[[11,3,8],[7,10,6],[0,14,6],[0,14,6]],[[13,10,12],[10,6,0],[12,5,14],[13,0,4]],[[14,0,11],[1,11,3],[7,2,14],[14,9,7]],[[3,10,15],[0,8,3],[14,15,1],[15,11,14]],[[0,3,6],[12,1,7],[9,12,3],[15,5,1]],[[15,2,14],[8,4,3],[12,9,13],[9,7,11]],[[11,4,9],[4,14,12],[6,14,8],[10,9,15]],[[3,7,2],[14,5,9],[2,15,4],[0,15,8]],[[11,12,2],[13,15,8],[13,8,14],[4,5,13]],[[1,2,3],[4,9,11],[12,13,0],[15,11,10]],[[2,4,1],[7,5,15],[3,8,14],[7,13,11]],[[1,6,10],[0,11,12],[15,0,13],[0,6,8]],[[11,10,5],[9,8,6],[10,4,12],[6,13,14]],[[7,12,10],[8,2,0],[15,2,9],[2,7,4]]]
YW = 17
def setup_inputs(rng):
    return {"x": rng.standard_normal((N, 128, T), dtype=np.float32)}
def reference(x):
    y = np.full((N, 128, YW), np.nan, x.dtype)
    fill = [0] * N
    for r in range(N):
        for t in range(T):
            for e in ROUTE[r][t]:
                y[e][:, fill[e]] = x[r][:, t]
                fill[e] += 1
    return {"y": y}

@@ -1,0 +1,103 @@
+from concourse.bass import DstId, RemoteDMATransfer
+
+SCRATCH = {
+    "xs": ("sbuf", [128, 4], "float32"),
+    "land": ("sbuf", [128, 17], "float32"),
+    "relay": ("sbuf", [128, 4], "float32"),
+}
+SEMAPHORES = ["loaded", "own", "arrived", "sent", "stored"]
+
+H1_CORE = 2
+H2_CORE = 3
+ENG = 2
+
+
+def plan(T):
+    route = T.tables["ROUTE"]
+    n = len(route)
+    col = [dict() for _ in range(n)]
+    for r in range(n):
+        for t in range(len(route[r])):
+            for e in route[r][t]:
+                col[e][(r, t)] = len(col[e])
+    return route, col
+
+
+def fan_out(g, T, topo, items, local_sem):
+    transfers = []
+    for k, (src, dsts) in enumerate(items):
+        ids = []
+        for c, _ in dsts:
+            rid, pid, _se = topo.addr(c)
+            ids.append(DstId(rid=rid, pnc=pid))
+        transfers.append(RemoteDMATransfer(dst_ids=ids, dma_engine_mask=((1 << ENG) - 1) << (ENG * k),
+                                           remote_sem=T.sem.arrived, srcs=[src], dsts=[ap for _, ap in dsts]))
+    if transfers:
+        g.remote_dma_fused(transfers, local_sem=local_sem)
+    return ENG * len(transfers)
+
+
+def rank_program(g, core, T, topo):
+    route, col = plan(T)
+    cores = T.cores
+    chip, k = topo.chip(core), core % 8
+    rank = T.rank_of(core)
+
+    def crossing(r):
+        return [t for t in range(len(route[r])) if any((e ^ r) & 1 for e in route[r][t])]
+
+    if rank is not None:
+        r = rank
+        h1 = chip * 8 + H1_CORE
+        g.sync.dma_start(T.xs[:], T.x[:]).then_inc(T.sem.loaded, 16)
+        g.wait_ge(T.sem.loaded, 16)
+        cross = crossing(r)
+        items = []
+        for t in range(len(route[r])):
+            dsts = [(cores[e], T.land[:, col[e][(r, t)]:col[e][(r, t)] + 1])
+                    for e in route[r][t] if e != r and not (e ^ r) & 1]
+            if t in cross:
+                i = cross.index(t)
+                dsts.append((h1, T.relay[:, i:i + 1]))
+            if dsts:
+                items.append((T.xs[:, t:t + 1], dsts))
+        sent = fan_out(g, T, topo, items, T.sem.sent)
+        mine = [t for t in range(len(route[r])) if r in route[r][t]]
+        if mine:
+            g.sync.wait_ge(T.sem.loaded, 16)
+            for t in mine:
+                c = col[r][(r, t)]
+                g.sync.dma_start(T.land[:, c:c + 1], T.xs[:, t:t + 1]).then_inc(T.sem.own, 16)
+            g.wait_ge(T.sem.own, 16 * len(mine))
+        count = len(col[r])
+        g.wait_ge(T.sem.arrived, ENG * (count - len(mine)))
+        g.dma_start(T.y[:, 0:count], T.land[:, 0:count]).then_inc(T.sem.stored, 16)
+        g.wait_ge(T.sem.sent, sent)
+        g.wait_ge(T.sem.stored, 16)
+        return
+
+    if k == H1_CORE:
+        r = chip
+        n = len(crossing(r))
+        if n == 0:
+            return
+        h2 = (chip ^ 1) * 8 + H2_CORE
+        rid, pid, _se = topo.addr(h2)
+        g.wait_ge(T.sem.arrived, ENG * n)
+        g.remote_dma(T.relay[:, 0:n], T.relay[:, 0:n], T.sem.arrived, T.sem.sent, pid, rid, 0xFF)
+        g.wait_ge(T.sem.sent, 8)
+        return
+
+    if k == H2_CORE:
+        r = chip ^ 1
+        cross = crossing(r)
+        if not cross:
+            return
+        g.wait_ge(T.sem.arrived, 8)
+        items = []
+        for i, t in enumerate(cross):
+            dsts = [(cores[e], T.land[:, col[e][(r, t)]:col[e][(r, t)] + 1]) for e in route[r][t] if (e ^ r) & 1]
+            items.append((T.relay[:, i:i + 1], dsts))
+        sent = fan_out(g, T, topo, items, T.sem.sent)
+        g.wait_ge(T.sem.sent, sent)
+        return

@@ -3,101 +3,191 @@ from concourse.bass import DstId, RemoteDMATransfer
 SCRATCH = {
     "xs": ("sbuf", [128, 4], "float32"),
     "land": ("sbuf", [128, 17], "float32"),
-    "relay": ("sbuf", [128, 4], "float32"),
+    "relay": ("sbuf", [128, 8], "float32"),
 }
 SEMAPHORES = ["loaded", "own", "arrived", "sent", "stored"]
 
-H1_CORE = 2
-H2_CORE = 3
-ENG = 2
+RK = 5
+S = (6, 2)
+G = (7, 3)
+F = (4, 0)
+
+CHOICE = [[17, 17, 13, 6], [17, 32, 2, 17], [16, 17, 2, 21], [5, 16, 38, 32], [8, 21, 13, 42], [5, 17, 9, 22],
+          [5, 22, 35, 19], [39, 21, 6, 17], [17, 21, 7, 14], [13, 7, 42, 14], [5, 17, 14, 19], [7, 15, 19, 7],
+          [3, 11, 4, 10], [30, 16, 1, 10], [16, 12, 7, 16], [34, 15, 8, 28]]
+
+CACHE = {}
 
 
-def plan(T):
-    route = T.tables["ROUTE"]
+def product(values, n):
+    out = [()]
+    for _ in range(n):
+        out = [p + (v,) for p in out for v in values]
+    return out
+
+
+def ways(route, r, t):
+    experts = route[r][t]
+    near = [e for e in experts if e != r and not (e ^ r) & 1]
+    far = [e for e in experts if (e ^ r) & 1]
+    me = r * 8 + RK
+    cross = []
+    if not far:
+        cross.append(([], None))
+    else:
+        for dies in product((0, 1), len(far)):
+            cross.append(([(r * 8 + S[d], e * 8 + RK) for e, d in zip(far, dies)], None))
+        if len(far) > 1:
+            for dm in (0, 1):
+                for df in (0, 1):
+                    f = (r ^ 1) * 8 + F[df]
+                    cross.append(([(r * 8 + S[dm], f)] + [(f, e * 8 + RK) for e in far], None))
+        for e in far:
+            p = e ^ 1
+            if p == r:
+                continue
+            for dm in (0, 1):
+                gate = p * 8 + G[dm]
+                head = [(me, gate)]
+                if p in near:
+                    head.append((gate, p * 8 + RK))
+                if len(far) == 1:
+                    cross.append((head + [(gate, e * 8 + RK)], p))
+                else:
+                    for df in (0, 1):
+                        f = e * 8 + F[df]
+                        cross.append((head + [(gate, f)] + [(f, q * 8 + RK) for q in far], p))
+    out = []
+    for writes, served in cross:
+        rest = [e for e in near if e != served]
+        if r in experts:
+            rest = rest + [r]
+        for senders in product((RK, S[0], S[1]), len(rest)):
+            out.append(writes + [(r * 8 + k, e * 8 + RK) for e, k in zip(rest, senders)])
+    return out
+
+
+def share_engines(loads, first, n):
+    eng = [1] * len(loads)
+    while True:
+        j = max(range(len(loads)), key=lambda i: (loads[i] / eng[i], -i))
+        if sum(eng) + eng[j] > n:
+            break
+        eng[j] *= 2
+    masks, at = [], first
+    for e in eng:
+        masks.append((((1 << e) - 1) << at, e))
+        at += e
+    return masks
+
+
+def build(route, choice):
     n = len(route)
     col = [dict() for _ in range(n)]
+    out = {}
+    slot, copies, calls, expect = {}, {}, {}, {}
     for r in range(n):
         for t in range(len(route[r])):
             for e in route[r][t]:
                 col[e][(r, t)] = len(col[e])
-    return route, col
-
-
-def fan_out(g, T, topo, items, local_sem):
-    transfers = []
-    for k, (src, dsts) in enumerate(items):
-        ids = []
-        for c, _ in dsts:
-            rid, pid, _se = topo.addr(c)
-            ids.append(DstId(rid=rid, pnc=pid))
-        transfers.append(RemoteDMATransfer(dst_ids=ids, dma_engine_mask=((1 << ENG) - 1) << (ENG * k),
-                                           remote_sem=T.sem.arrived, srcs=[src], dsts=[ap for _, ap in dsts]))
-    if transfers:
-        g.remote_dma_fused(transfers, local_sem=local_sem)
-    return ENG * len(transfers)
+            w = ways(route, r, t)
+            for a, b in w[choice[r][t] % len(w)]:
+                if a == b:
+                    copies.setdefault(a, []).append((r, t))
+                    continue
+                out.setdefault(a, {}).setdefault((r, t), []).append(b)
+                if b % 8 != RK:
+                    slot.setdefault(b, {})[(r, t)] = len(slot.get(b, {}))
+    for r in range(n):
+        hand = [r * 8 + k for k in S if r * 8 + k in out]
+        if hand:
+            calls.setdefault(r * 8 + RK, []).append([(None, hand, 0xFFFF, 16)])
+    for a in sorted(out):
+        away, home = [], []
+        for tok in sorted(out[a]):
+            far = [b for b in out[a][tok] if b // 8 != a // 8]
+            here = [b for b in out[a][tok] if b // 8 == a // 8]
+            if far:
+                away.append((tok, far))
+            if here:
+                home.append((tok, here))
+        while away or home:
+            now_a, away = away[:8], away[8:]
+            now_h, home = home[:8], home[8:]
+            call = []
+            if now_a:
+                for (tok, dst), (m, e) in zip(now_a, share_engines([len(d) for _, d in now_a], 0, 8)):
+                    call.append((tok, dst, m, e))
+            if now_h:
+                lo, width = (8, 8) if now_a else (0, 16)
+                for (tok, dst), (m, e) in zip(now_h, share_engines([len(d) for _, d in now_h], lo, width)):
+                    call.append((tok, dst, m, e))
+            calls.setdefault(a, []).append(call)
+    for a in calls:
+        for call in calls[a]:
+            for _tok, dst, _m, e in call:
+                for b in dst:
+                    expect[b] = expect.get(b, 0) + e
+    return {"col": col, "slot": slot, "calls": calls, "copies": copies, "expect": expect}
 
 
 def rank_program(g, core, T, topo):
-    route, col = plan(T)
-    cores = T.cores
-    chip, k = topo.chip(core), core % 8
-    rank = T.rank_of(core)
+    route = T.tables["ROUTE"]
+    if "plan" not in CACHE:
+        CACHE["plan"] = build(route, CHOICE)
+    plan = CACHE["plan"]
+    col, slot = plan["col"], plan["slot"]
+    calls = plan["calls"].get(core, [])
+    expect = plan["expect"].get(core, 0)
+    ntok = len(route[0])
 
-    def crossing(r):
-        return [t for t in range(len(route[r])) if any((e ^ r) & 1 for e in route[r][t])]
+    def at(c, tok):
+        k = c % 8
+        if tok is None:
+            return T.xs[:, 0:ntok] if k == RK else T.relay[:, 0:ntok]
+        r, t = tok
+        if k == RK:
+            if c == core:
+                return T.xs[:, t:t + 1]
+            i = col[c // 8][tok]
+            return T.land[:, i:i + 1]
+        i = t if k in S else slot[c][tok]
+        return T.relay[:, i:i + 1]
 
-    if rank is not None:
-        r = rank
-        h1 = chip * 8 + H1_CORE
-        g.sync.dma_start(T.xs[:], T.x[:]).then_inc(T.sem.loaded, 16)
-        g.wait_ge(T.sem.loaded, 16)
-        cross = crossing(r)
-        items = []
-        for t in range(len(route[r])):
-            dsts = [(cores[e], T.land[:, col[e][(r, t)]:col[e][(r, t)] + 1])
-                    for e in route[r][t] if e != r and not (e ^ r) & 1]
-            if t in cross:
-                i = cross.index(t)
-                dsts.append((h1, T.relay[:, i:i + 1]))
-            if dsts:
-                items.append((T.xs[:, t:t + 1], dsts))
-        sent = fan_out(g, T, topo, items, T.sem.sent)
-        mine = [t for t in range(len(route[r])) if r in route[r][t]]
-        if mine:
-            g.sync.wait_ge(T.sem.loaded, 16)
-            for t in mine:
-                c = col[r][(r, t)]
-                g.sync.dma_start(T.land[:, c:c + 1], T.xs[:, t:t + 1]).then_inc(T.sem.own, 16)
-            g.wait_ge(T.sem.own, 16 * len(mine))
-        count = len(col[r])
-        g.wait_ge(T.sem.arrived, ENG * (count - len(mine)))
-        g.dma_start(T.y[:, 0:count], T.land[:, 0:count]).then_inc(T.sem.stored, 16)
-        g.wait_ge(T.sem.sent, sent)
-        g.wait_ge(T.sem.stored, 16)
-        return
+    def send():
+        total = 0
+        for call in calls:
+            transfers = []
+            for tok, dst, m, e in call:
+                ids = [DstId(rid=topo.addr(b)[0], pnc=topo.addr(b)[1]) for b in dst]
+                transfers.append(RemoteDMATransfer(dst_ids=ids, dma_engine_mask=m, remote_sem=T.sem.arrived,
+                                                   srcs=[at(core, tok)], dsts=[at(b, tok) for b in dst]))
+                total += e
+            g.remote_dma_fused(transfers, local_sem=T.sem.sent)
+        return total
 
-    if k == H1_CORE:
-        r = chip
-        n = len(crossing(r))
-        if n == 0:
+    if T.rank_of(core) is None:
+        if not calls:
             return
-        h2 = (chip ^ 1) * 8 + H2_CORE
-        rid, pid, _se = topo.addr(h2)
-        g.wait_ge(T.sem.arrived, ENG * n)
-        g.remote_dma(T.relay[:, 0:n], T.relay[:, 0:n], T.sem.arrived, T.sem.sent, pid, rid, 0xFF)
-        g.wait_ge(T.sem.sent, 8)
+        g.wait_ge(T.sem.arrived, expect)
+        g.wait_ge(T.sem.sent, send())
         return
 
-    if k == H2_CORE:
-        r = chip ^ 1
-        cross = crossing(r)
-        if not cross:
-            return
-        g.wait_ge(T.sem.arrived, 8)
-        items = []
-        for i, t in enumerate(cross):
-            dsts = [(cores[e], T.land[:, col[e][(r, t)]:col[e][(r, t)] + 1]) for e in route[r][t] if (e ^ r) & 1]
-            items.append((T.relay[:, i:i + 1], dsts))
-        sent = fan_out(g, T, topo, items, T.sem.sent)
+    r = T.rank_of(core)
+    q = g.sync
+    q.dma_start(T.xs[:], T.x[:]).then_inc(T.sem.loaded, 16)
+    g.wait_ge(T.sem.loaded, 16)
+    sent = send()
+    mine = plan["copies"].get(core, [])
+    if mine:
+        q.wait_ge(T.sem.loaded, 16)
+        for tok in mine:
+            i = col[r][tok]
+            q.dma_start(T.land[:, i:i + 1], T.xs[:, tok[1]:tok[1] + 1]).then_inc(T.sem.own, 16)
+        q.wait_ge(T.sem.own, 16 * len(mine))
+    count = len(col[r])
+    q.wait_ge(T.sem.arrived, expect)
+    q.dma_start(T.y[:, 0:count], T.land[:, 0:count]).then_inc(T.sem.stored, 16)
+    if sent:
         g.wait_ge(T.sem.sent, sent)
-        return
+    g.wait_ge(T.sem.stored, 16)

@@ -3,7 +3,7 @@ from concourse.bass import DstId, RemoteDMATransfer
 SCRATCH = {
     "xs": ("sbuf", [128, 4], "float32"),
     "land": ("sbuf", [128, 17], "float32"),
-    "relay": ("sbuf", [128, 8], "float32"),
+    "relay": ("sbuf", [128, 64], "float32"),
 }
 SEMAPHORES = ["loaded", "own", "arrived", "sent", "stored"]
 
@@ -12,9 +12,9 @@ S = (6, 2)
 G = (7, 3)
 F = (4, 0)
 
-CHOICE = [[17, 17, 13, 6], [17, 32, 2, 17], [16, 17, 2, 21], [5, 16, 38, 32], [8, 21, 13, 42], [5, 17, 9, 22],
-          [5, 22, 35, 19], [39, 21, 6, 17], [17, 21, 7, 14], [13, 7, 42, 14], [5, 17, 14, 19], [7, 15, 19, 7],
-          [3, 11, 4, 10], [30, 16, 1, 10], [16, 12, 7, 16], [34, 15, 8, 28]]
+CHOICE = [[23, 8, 16, 3], [35, 17, 4, 15], [16, 22, 24, 26], [1, 18, 40, 28], [4, 22, 17, 34], [7, 23, 15, 23],
+          [7, 17, 22, 16], [39, 15, 4, 23], [16, 23, 16, 23], [17, 4, 41, 20], [16, 14, 5, 23], [5, 17, 19, 3],
+          [16, 11, 7, 8], [32, 23, 8, 11], [13, 10, 16, 15], [25, 12, 4, 34]]
 
 CACHE = {}
 
@@ -98,34 +98,44 @@ def build(route, choice):
                 out.setdefault(a, {}).setdefault((r, t), []).append(b)
                 if b % 8 != RK:
                     slot.setdefault(b, {})[(r, t)] = len(slot.get(b, {}))
-    for r in range(n):
-        hand = [r * 8 + k for k in S if r * 8 + k in out]
-        if hand:
-            calls.setdefault(r * 8 + RK, []).append([(None, hand, 0xFFFF, 16)])
+    sends = {}
     for a in sorted(out):
-        away, home = [], []
-        for tok in sorted(out[a]):
-            far = [b for b in out[a][tok] if b // 8 != a // 8]
-            here = [b for b in out[a][tok] if b // 8 == a // 8]
-            if far:
-                away.append((tok, far))
-            if here:
-                home.append((tok, here))
-        while away or home:
-            now_a, away = away[:8], away[8:]
-            now_h, home = home[:8], home[8:]
-            call = []
-            if now_a:
-                for (tok, dst), (m, e) in zip(now_a, share_engines([len(d) for _, d in now_a], 0, 8)):
-                    call.append((tok, dst, m, e))
-            if now_h:
-                lo, width = (8, 8) if now_a else (0, 16)
-                for (tok, dst), (m, e) in zip(now_h, share_engines([len(d) for _, d in now_h], lo, width)):
-                    call.append((tok, dst, m, e))
-            calls.setdefault(a, []).append(call)
+        sends[a] = [(tok, 1, out[a][tok]) for tok in sorted(out[a])]
+    for r in range(n):
+        hand = {}
+        for k in S:
+            if r * 8 + k in out:
+                ts = sorted(t for _, t in out[r * 8 + k])
+                hand.setdefault((ts[0], ts[-1] - ts[0] + 1), []).append(r * 8 + k)
+        for t0, width in sorted(hand):
+            sends.setdefault(r * 8 + RK, []).append(((r, t0), width, hand[(t0, width)]))
+    for a in sorted(sends):
+        for width in sorted(set(w for _, w, _ in sends[a]), reverse=True):
+            away, home = [], []
+            for tok, w, dst in sends[a]:
+                if w != width:
+                    continue
+                far = [b for b in dst if b // 8 != a // 8]
+                here = [b for b in dst if b // 8 == a // 8]
+                if far:
+                    away.append((tok, far))
+                if here:
+                    home.append((tok, here))
+            while away or home:
+                now_a, away = away[:8], away[8:]
+                now_h, home = home[:8], home[8:]
+                call = []
+                if now_a:
+                    for (tok, dst), (m, e) in zip(now_a, share_engines([len(d) for _, d in now_a], 0, 8)):
+                        call.append((tok, width, dst, m, e))
+                if now_h:
+                    lo, room = (8, 8) if now_a else (0, 16)
+                    for (tok, dst), (m, e) in zip(now_h, share_engines([len(d) for _, d in now_h], lo, room)):
+                        call.append((tok, width, dst, m, e))
+                calls.setdefault(a, []).append(call)
     for a in calls:
         for call in calls[a]:
-            for _tok, dst, _m, e in call:
+            for _tok, _w, dst, _m, e in call:
                 for b in dst:
                     expect[b] = expect.get(b, 0) + e
     return {"col": col, "slot": slot, "calls": calls, "copies": copies, "expect": expect}
@@ -139,29 +149,25 @@ def rank_program(g, core, T, topo):
     col, slot = plan["col"], plan["slot"]
     calls = plan["calls"].get(core, [])
     expect = plan["expect"].get(core, 0)
-    ntok = len(route[0])
 
-    def at(c, tok):
+    def at(c, tok, width):
         k = c % 8
-        if tok is None:
-            return T.xs[:, 0:ntok] if k == RK else T.relay[:, 0:ntok]
-        r, t = tok
+        if k == RK and c == core:
+            return T.xs[:, tok[1]:tok[1] + width]
         if k == RK:
-            if c == core:
-                return T.xs[:, t:t + 1]
             i = col[c // 8][tok]
-            return T.land[:, i:i + 1]
-        i = t if k in S else slot[c][tok]
-        return T.relay[:, i:i + 1]
+            return T.land[:, i:i + width]
+        i = tok[1] if k in S else slot[c][tok]
+        return T.relay[:, i:i + width]
 
     def send():
         total = 0
         for call in calls:
             transfers = []
-            for tok, dst, m, e in call:
+            for tok, width, dst, m, e in call:
                 ids = [DstId(rid=topo.addr(b)[0], pnc=topo.addr(b)[1]) for b in dst]
                 transfers.append(RemoteDMATransfer(dst_ids=ids, dma_engine_mask=m, remote_sem=T.sem.arrived,
-                                                   srcs=[at(core, tok)], dsts=[at(b, tok) for b in dst]))
+                                                   srcs=[at(core, tok, width)], dsts=[at(b, tok, width) for b in dst]))
                 total += e
             g.remote_dma_fused(transfers, local_sem=T.sem.sent)
         return total

from concourse.bass import DstId, RemoteDMATransfer

SCRATCH = {
    "xs": ("sbuf", [128, 4], "float32"),
    "land": ("sbuf", [128, 17], "float32"),
    "relay": ("sbuf", [128, 64], "float32"),
}
SEMAPHORES = ["loaded", "own", "arrived", "sent", "stored"]

RK = 5
S = (6, 2)
G = (7, 3)
F = (4, 0)

CHOICE = [[23, 8, 16, 3], [35, 17, 4, 15], [16, 22, 24, 26], [1, 18, 40, 28], [4, 22, 17, 34], [7, 23, 15, 23],
          [7, 17, 22, 16], [39, 15, 4, 23], [16, 23, 16, 23], [17, 4, 41, 20], [16, 14, 5, 23], [5, 17, 19, 3],
          [16, 11, 7, 8], [32, 23, 8, 11], [13, 10, 16, 15], [25, 12, 4, 34]]

CACHE = {}


def product(values, n):
    out = [()]
    for _ in range(n):
        out = [p + (v,) for p in out for v in values]
    return out


def ways(route, r, t):
    experts = route[r][t]
    near = [e for e in experts if e != r and not (e ^ r) & 1]
    far = [e for e in experts if (e ^ r) & 1]
    me = r * 8 + RK
    cross = []
    if not far:
        cross.append(([], None))
    else:
        for dies in product((0, 1), len(far)):
            cross.append(([(r * 8 + S[d], e * 8 + RK) for e, d in zip(far, dies)], None))
        if len(far) > 1:
            for dm in (0, 1):
                for df in (0, 1):
                    f = (r ^ 1) * 8 + F[df]
                    cross.append(([(r * 8 + S[dm], f)] + [(f, e * 8 + RK) for e in far], None))
        for e in far:
            p = e ^ 1
            if p == r:
                continue
            for dm in (0, 1):
                gate = p * 8 + G[dm]
                head = [(me, gate)]
                if p in near:
                    head.append((gate, p * 8 + RK))
                if len(far) == 1:
                    cross.append((head + [(gate, e * 8 + RK)], p))
                else:
                    for df in (0, 1):
                        f = e * 8 + F[df]
                        cross.append((head + [(gate, f)] + [(f, q * 8 + RK) for q in far], p))
    out = []
    for writes, served in cross:
        rest = [e for e in near if e != served]
        if r in experts:
            rest = rest + [r]
        for senders in product((RK, S[0], S[1]), len(rest)):
            out.append(writes + [(r * 8 + k, e * 8 + RK) for e, k in zip(rest, senders)])
    return out


def share_engines(loads, first, n):
    eng = [1] * len(loads)
    while True:
        j = max(range(len(loads)), key=lambda i: (loads[i] / eng[i], -i))
        if sum(eng) + eng[j] > n:
            break
        eng[j] *= 2
    masks, at = [], first
    for e in eng:
        masks.append((((1 << e) - 1) << at, e))
        at += e
    return masks


def build(route, choice):
    n = len(route)
    col = [dict() for _ in range(n)]
    out = {}
    slot, copies, calls, expect = {}, {}, {}, {}
    for r in range(n):
        for t in range(len(route[r])):
            for e in route[r][t]:
                col[e][(r, t)] = len(col[e])
            w = ways(route, r, t)
            for a, b in w[choice[r][t] % len(w)]:
                if a == b:
                    copies.setdefault(a, []).append((r, t))
                    continue
                out.setdefault(a, {}).setdefault((r, t), []).append(b)
                if b % 8 != RK:
                    slot.setdefault(b, {})[(r, t)] = len(slot.get(b, {}))
    sends = {}
    for a in sorted(out):
        sends[a] = [(tok, 1, out[a][tok]) for tok in sorted(out[a])]
    for r in range(n):
        hand = {}
        for k in S:
            if r * 8 + k in out:
                ts = sorted(t for _, t in out[r * 8 + k])
                hand.setdefault((ts[0], ts[-1] - ts[0] + 1), []).append(r * 8 + k)
        for t0, width in sorted(hand):
            sends.setdefault(r * 8 + RK, []).append(((r, t0), width, hand[(t0, width)]))
    for a in sorted(sends):
        for width in sorted(set(w for _, w, _ in sends[a]), reverse=True):
            away, home = [], []
            for tok, w, dst in sends[a]:
                if w != width:
                    continue
                far = [b for b in dst if b // 8 != a // 8]
                here = [b for b in dst if b // 8 == a // 8]
                if far:
                    away.append((tok, far))
                if here:
                    home.append((tok, here))
            while away or home:
                now_a, away = away[:8], away[8:]
                now_h, home = home[:8], home[8:]
                call = []
                if now_a:
                    for (tok, dst), (m, e) in zip(now_a, share_engines([len(d) for _, d in now_a], 0, 8)):
                        call.append((tok, width, dst, m, e))
                if now_h:
                    lo, room = (8, 8) if now_a else (0, 16)
                    for (tok, dst), (m, e) in zip(now_h, share_engines([len(d) for _, d in now_h], lo, room)):
                        call.append((tok, width, dst, m, e))
                calls.setdefault(a, []).append(call)
    for a in calls:
        for call in calls[a]:
            for _tok, _w, dst, _m, e in call:
                for b in dst:
                    expect[b] = expect.get(b, 0) + e
    return {"col": col, "slot": slot, "calls": calls, "copies": copies, "expect": expect}


def rank_program(g, core, T, topo):
    route = T.tables["ROUTE"]
    if "plan" not in CACHE:
        CACHE["plan"] = build(route, CHOICE)
    plan = CACHE["plan"]
    col, slot = plan["col"], plan["slot"]
    calls = plan["calls"].get(core, [])
    expect = plan["expect"].get(core, 0)

    def at(c, tok, width):
        k = c % 8
        if k == RK and c == core:
            return T.xs[:, tok[1]:tok[1] + width]
        if k == RK:
            i = col[c // 8][tok]
            return T.land[:, i:i + width]
        i = tok[1] if k in S else slot[c][tok]
        return T.relay[:, i:i + width]

    def send():
        total = 0
        for call in calls:
            transfers = []
            for tok, width, dst, m, e in call:
                ids = [DstId(rid=topo.addr(b)[0], pnc=topo.addr(b)[1]) for b in dst]
                transfers.append(RemoteDMATransfer(dst_ids=ids, dma_engine_mask=m, remote_sem=T.sem.arrived,
                                                   srcs=[at(core, tok, width)], dsts=[at(b, tok, width) for b in dst]))
                total += e
            g.remote_dma_fused(transfers, local_sem=T.sem.sent)
        return total

    if T.rank_of(core) is None:
        if not calls:
            return
        g.wait_ge(T.sem.arrived, expect)
        g.wait_ge(T.sem.sent, send())
        return

    r = T.rank_of(core)
    q = g.sync
    q.dma_start(T.xs[:], T.x[:]).then_inc(T.sem.loaded, 16)
    g.wait_ge(T.sem.loaded, 16)
    sent = send()
    mine = plan["copies"].get(core, [])
    if mine:
        q.wait_ge(T.sem.loaded, 16)
        for tok in mine:
            i = col[r][tok]
            q.dma_start(T.land[:, i:i + 1], T.xs[:, tok[1]:tok[1] + 1]).then_inc(T.sem.own, 16)
        q.wait_ge(T.sem.own, 16 * len(mine))
    count = len(col[r])
    q.wait_ge(T.sem.arrived, expect)
    q.dma_start(T.y[:, 0:count], T.land[:, 0:count]).then_inc(T.sem.stored, 16)
    if sent:
        g.wait_ge(T.sem.sent, sent)
    g.wait_ge(T.sem.stored, 16)
